import numpy as np
import ml_dtypes


def mxq(x, axis, fmt="e4m3"):
    dtype, down = {"e4m3": (ml_dtypes.float8_e4m3fn, 7), "e5m2": (ml_dtypes.float8_e5m2, 14)}[fmt]
    v = np.moveaxis(np.asarray(x, np.float32).astype(ml_dtypes.bfloat16).astype(np.float64), axis, -1)
    blocks = v.reshape(v.shape[:-1] + (-1, 32))
    amax = np.abs(blocks).max(-1, keepdims=True)
    byte = np.maximum(np.where(amax > 0, np.frexp(amax)[1] - 1 + 127, 0) - down, 1)
    scale = np.exp2(byte - 127.0)
    codes = (blocks / scale).astype(np.float32).astype(dtype).astype(np.float64)
    return np.moveaxis((codes * scale).reshape(v.shape), -1, axis)


WIDE = False


def mx_kscale(k):
    if not WIDE:
        return np.ones(k)
    levels = np.array([10, -10, 5, -5, 0])
    if k % 512:
        return np.exp2(np.random.permutation(np.resize(levels, k // 32))).repeat(32)
    a = np.empty((k // 512, 16))
    for p in range(k // 512):
        a[p, :8] = np.random.permutation(np.resize(levels, 8))
        for g in range(8):
            far = levels[np.abs(levels - a[p, g]) >= 10]
            a[p, g + 8] = far[np.random.randint(len(far))]
    return np.exp2(a.ravel()).repeat(32)


def f64(x):
    return np.asarray(x).astype(np.float64)


def striped(idx):
    return np.tile(idx.reshape(-1, 16).T, (8, 1)).astype(np.uint16)


def unstriped(offs):
    return offs[:16].T.reshape(-1).astype(np.int64)


def pack_weight(w):
    k, n = w.shape
    w = f64(np.asarray(w, np.float32).astype(ml_dtypes.bfloat16)).reshape(k // 32, 32, n)
    amax = np.abs(w).max(1)
    byte = np.clip(np.where(amax > 0, np.frexp(amax)[1] - 1 + 127 - 7, 1), 1, 254)
    scaled = (w * np.exp2(127.0 - byte)[:, None, :]).reshape(k, n).astype(np.float32)
    words = np.ascontiguousarray(scaled.reshape(k // 512, 128, 4, n).transpose(0, 1, 3, 2)).astype(ml_dtypes.float8_e4m3fn).view(np.uint8)
    return words, np.ascontiguousarray(byte.astype(np.uint8).reshape(k // 512, 16, n))


def unpack_weight(words, scales):
    g, p, n, _ = words.shape
    vals = np.ascontiguousarray(words).view(ml_dtypes.float8_e4m3fn).astype(np.float64) * np.repeat(np.exp2(scales.astype(np.float64) - 127.0), 8, axis=1)[..., None]
    return vals.transpose(0, 1, 3, 2).reshape(g * 512, n)


def relu(v):
    return np.maximum(v, 0.0)


K, T, S, V, H, N = 1024, 1024, 512, 256, 512, 128


def setup_inputs():
    n = np.random.standard_normal
    s = mx_kscale(K)[:, None]
    u = mx_kscale(H)
    packed_xT = pack_weight(n((K, T)) * s)
    packed_w2 = pack_weight(n((H, N)) / np.sqrt(H) / u[:, None])
    return {
        "x_words": packed_xT[0],
        "x_scales": packed_xT[1],
        "w1": (n((K, H)) / np.sqrt(K) / s * u).astype(np.float32),
        "w2_words": packed_w2[0],
        "w2_scales": packed_w2[1],
        "offs": striped(np.random.permutation(T)[:S]),
    }


def reference(x_words, x_scales, w1, w2_words, w2_scales, offs):
    xq = unpack_weight(x_words, x_scales)[:, unstriped(offs)]
    h = relu(mxq(f64(w1), 0, "e4m3").T @ xq)
    z = np.abs(h[:, :V] - h[:, V:2 * V])
    return unpack_weight(w2_words, w2_scales).T @ mxq(z, 0, "e4m3")

@@ -1,0 +1,179 @@
+from contextlib import ExitStack
+
+import concourse.mybir as mybir
+
+K, T, S, V, H, N = 1024, 1024, 512, 256, 512, 128
+FLOPS = 2 * K * H * S + 2 * H * N * V
+
+F32 = mybir.dt.float32
+BF16 = mybir.dt.bfloat16
+I32 = mybir.dt.int32
+U32 = mybir.dt.uint32
+U16 = mybir.dt.uint16
+U8 = mybir.dt.uint8
+FP8X4 = mybir.dt.float8_e4m3fn_x4
+ACT = mybir.ActivationFunctionType
+ALU = mybir.AluOpType
+
+P = 128
+PACK = 4
+PASSES = K // (P * PACK)
+C = 128
+CHUNKS = V // C
+
+FIRST_AT = (0, 128)
+SECOND_AT = (128, 0)
+
+
+def tile_picked_siam_abs_p_kernel(
+    tc, x_words, x_scales, w1, w2_words, w2_scales, offs, out
+):
+    nc = tc.nc
+    with ExitStack() as ctx:
+        keep = ctx.enter_context(tc.tile_pool(name="keep", bufs=1))
+        psum = ctx.enter_context(tc.psum_pool(name="psum", bufs=1))
+
+        offsets = keep.tile([P, S // 16], U16, name="offsets")
+        xs = keep.tile([P, T], U8, name="xs", align_bytes=64)
+        xw = [keep.tile([P, T], U32, name="xw%d" % g, align_bytes=64) for g in range(PASSES)]
+        raw = [keep.tile([P, PACK, H], F32, name="raw%d" % g, align_bytes=64) for g in range(PASSES)]
+        grouped = [
+            [keep.tile([P, H * PACK // 2], BF16, name="grouped%d_%d" % (g, h), align_bytes=64) for h in range(2)]
+            for g in range(PASSES)
+        ]
+        w1c = [keep.tile([P, H], U32, name="w1c%d" % g, align_bytes=64) for g in range(PASSES)]
+        w1s = [keep.tile([P, H], U8, name="w1s%d" % g, align_bytes=64) for g in range(PASSES)]
+        gw = [keep.tile([P, S], U32, name="gw%d" % g, align_bytes=64) for g in range(PASSES)]
+        gs = keep.tile([P, S], U8, name="gs", align_bytes=64)
+        w2w = keep.tile([P, N], U32, name="w2w", align_bytes=64)
+        w2s = keep.tile([P, N], U8, name="w2s", align_bytes=64)
+
+        def load_w1(g):
+            rows = w1[g * P * PACK : (g + 1) * P * PACK, :]
+            nc.sync.dma_start(out=raw[g][:], in_=rows.rearrange("(p j) c -> p j c", j=PACK))
+
+        def load_x(g):
+            src = x_words[g].rearrange("p n t -> p (n t)").bitcast(I32)
+            nc.sync.dma_start(out=xw[g][:].bitcast(I32), in_=src)
+
+        nc.gpsimd.memset(xs[:].bitcast(I32), 0)
+        nc.gpsimd.memset(w2s[:].bitcast(I32), 0)
+        nc.sync.dma_start(offsets[:], offs)
+        for q in range(4):
+            nc.sync.dma_start(
+                out=xs[32 * q : 32 * q + 4 * PASSES, :].bitcast(I32),
+                in_=x_scales[:, 4 * q : 4 * q + 4, :].bitcast(I32),
+            )
+        load_w1(0)
+        load_x(0)
+        load_w1(1)
+        load_x(1)
+        nc.sync.dma_start(
+            out=w2w[:].bitcast(I32), in_=w2_words[0].rearrange("p n t -> p (n t)").bitcast(I32)
+        )
+        for q in range(4):
+            nc.sync.dma_start(
+                out=w2s[32 * q : 32 * q + 4, :].bitcast(I32),
+                in_=w2_scales[0, 4 * q : 4 * q + 4, :].bitcast(I32),
+            )
+
+        def gather(dst, window, at, entry, count):
+            nc.vector.tensor_copy(
+                dst[:, at : at + count], window[:].indirect(offsets[:, entry // 16 : (entry + count) // 16])
+            )
+
+        def gather_all(dst, window):
+            gather(dst, window, 0, 0, C)
+            gather(dst, window, C, V, V)
+            gather(dst, window, 3 * C, C, C)
+
+        def interleave(g, h):
+            dst = grouped[g][h][:].rearrange("p (t m j) -> p m j t", t=2, j=PACK)
+            src = raw[g][:].rearrange("p j (m t) -> p m j t", t=PACK)[:, :, :, 2 * h : 2 * h + 2]
+            if h == 0:
+                nc.vector.tensor_copy(out=dst, in_=src)
+            else:
+                nc.scalar.activation(out=dst, in_=src, func=ACT.Copy)
+
+        def quantize_w1(g, h):
+            cols = slice(h * H // 2, (h + 1) * H // 2)
+            nc.vector.quantize_mx(out=w1c[g][:, cols].bitcast(FP8X4), scales=w1s[g][:, cols], in_=grouped[g][h][:])
+
+        banks = [
+            [psum.tile([P, 2 * C], F32, name="h%d_%d" % (c, t), tag="b%d_%d" % (c, t)) for t in range(PACK)]
+            for c in range(CHUNKS)
+        ]
+
+        def first_layer(g, c):
+            cols = slice(2 * C * c, 2 * C * (c + 1))
+            for t in range(PACK):
+                chan = slice(P * t, P * (t + 1))
+                nc.tensor.matmul_mx(
+                    out=banks[c][t][:],
+                    lhsT=w1c[g][:, chan].bitcast(FP8X4),
+                    lhsT_scale=w1s[g][:, chan],
+                    rhs=gw[g][:, cols].bitcast(FP8X4),
+                    rhs_scale=gs[4 * g : P, cols],
+                    start=(g == 0),
+                    stop=(g == PASSES - 1),
+                )
+
+        gather_all(gs, xs)
+        interleave(0, 0)
+        interleave(0, 1)
+        quantize_w1(0, 0)
+        quantize_w1(0, 1)
+        gather_all(gw[0], xw[0])
+        for c in range(CHUNKS):
+            first_layer(0, c)
+        interleave(1, 0)
+        interleave(1, 1)
+        quantize_w1(1, 0)
+        quantize_w1(1, 1)
+        for c in range(CHUNKS):
+            gather(gw[1], xw[1], 2 * C * c + FIRST_AT[c], C * c, C)
+            gather(gw[1], xw[1], 2 * C * c + SECOND_AT[c], V + C * c, C)
+        for c in range(CHUNKS):
+            first_layer(1, c)
+
+        diffs = []
+        for c in range(CHUNKS):
+            second = keep.tile([P, PACK, C], F32, name="second%d" % c)
+            diff = keep.tile([P, PACK, C], F32, name="diff%d" % c)
+            diffs.append(diff)
+            for t in range(PACK):
+                bank = banks[c][t]
+                nc.scalar.activation(
+                    out=second[:, t, :], in_=bank[:, SECOND_AT[c] : SECOND_AT[c] + C], func=ACT.Relu
+                )
+                nc.vector.scalar_tensor_tensor(
+                    out=diff[:, t, :],
+                    in0=bank[:, FIRST_AT[c] : FIRST_AT[c] + C],
+                    scalar=0.0,
+                    in1=second[:, t, :],
+                    op0=ALU.max,
+                    op1=ALU.subtract,
+                )
+        for c in range(CHUNKS):
+            z = keep.tile([P, C * PACK], BF16, name="z%d" % c, align_bytes=64)
+            zc = keep.tile([P, C], U32, name="zc%d" % c, align_bytes=64)
+            zs = keep.tile([P, C], U8, name="zs%d" % c, align_bytes=64)
+            nc.scalar.activation(
+                out=z[:].rearrange("p (u i t) -> p u t i", i=4, t=PACK),
+                in_=diffs[c][:].rearrange("p t (u i) -> p u t i", i=4),
+                func=ACT.Abs,
+            )
+            nc.vector.quantize_mx(out=zc[:].bitcast(FP8X4), scales=zs[:], in_=z[:])
+            acc = psum.tile([P, C], F32, name="acc%d" % c, tag="b0_%d" % c)
+            nc.tensor.matmul_mx(
+                out=acc[:],
+                lhsT=w2w[:].bitcast(FP8X4),
+                lhsT_scale=w2s[:],
+                rhs=zc[:].bitcast(FP8X4),
+                rhs_scale=zs[:],
+                start=True,
+                stop=True,
+            )
+            res = keep.tile([P, C], F32, name="res%d" % c)
+            nc.vector.tensor_copy(out=res[:], in_=acc[:])
+            nc.sync.dma_start(out=out[:, C * c : C * (c + 1)], in_=res[:])

@@ -20,6 +20,7 @@ PACK = 4
 PASSES = K // (P * PACK)
 C = 128
 CHUNKS = V // C
+VEC_ABS = (0, 64)
 
 FIRST_AT = (0, 128)
 SECOND_AT = (128, 0)
@@ -59,13 +60,13 @@ def tile_picked_siam_abs_p_kernel(
         nc.gpsimd.memset(xs[:].bitcast(I32), 0)
         nc.gpsimd.memset(w2s[:].bitcast(I32), 0)
         nc.sync.dma_start(offsets[:], offs)
+        load_x(0)
         for q in range(4):
             nc.sync.dma_start(
                 out=xs[32 * q : 32 * q + 4 * PASSES, :].bitcast(I32),
                 in_=x_scales[:, 4 * q : 4 * q + 4, :].bitcast(I32),
             )
         load_w1(0)
-        load_x(0)
         load_w1(1)
         load_x(1)
         nc.sync.dma_start(
@@ -88,8 +89,8 @@ def tile_picked_siam_abs_p_kernel(
             gather(dst, window, 3 * C, C, C)
 
         def interleave(g, h):
-            dst = grouped[g][h][:].rearrange("p (t m j) -> p m j t", t=2, j=PACK)
-            src = raw[g][:].rearrange("p j (m t) -> p m j t", t=PACK)[:, :, :, 2 * h : 2 * h + 2]
+            dst = grouped[g][h][:].rearrange("p (t m j) -> p m t j", t=2, j=PACK)
+            src = raw[g][:].rearrange("p j (m t) -> p m t j", t=PACK)[:, :, 2 * h : 2 * h + 2, :]
             if h == 0:
                 nc.vector.tensor_copy(out=dst, in_=src)
             else:
@@ -118,21 +119,24 @@ def tile_picked_siam_abs_p_kernel(
                     stop=(g == PASSES - 1),
                 )
 
+        def gather_chunk(c):
+            gather(gw[1], xw[1], 2 * C * c + FIRST_AT[c], C * c, C)
+            gather(gw[1], xw[1], 2 * C * c + SECOND_AT[c], V + C * c, C)
+
+        gather_all(gw[0], xw[0])
         gather_all(gs, xs)
         interleave(0, 0)
         interleave(0, 1)
         quantize_w1(0, 0)
         quantize_w1(0, 1)
-        gather_all(gw[0], xw[0])
         for c in range(CHUNKS):
             first_layer(0, c)
         interleave(1, 0)
         interleave(1, 1)
         quantize_w1(1, 0)
+        gather_chunk(0)
         quantize_w1(1, 1)
-        for c in range(CHUNKS):
-            gather(gw[1], xw[1], 2 * C * c + FIRST_AT[c], C * c, C)
-            gather(gw[1], xw[1], 2 * C * c + SECOND_AT[c], V + C * c, C)
+        gather_chunk(1)
         for c in range(CHUNKS):
             first_layer(1, c)
 
@@ -154,17 +158,31 @@ def tile_picked_siam_abs_p_kernel(
                     op0=ALU.max,
                     op1=ALU.subtract,
                 )
+        zs_bf = [keep.tile([P, C * PACK], BF16, name="z%d" % c, align_bytes=64) for c in range(CHUNKS)]
         for c in range(CHUNKS):
-            z = keep.tile([P, C * PACK], BF16, name="z%d" % c, align_bytes=64)
-            zc = keep.tile([P, C], U32, name="zc%d" % c, align_bytes=64)
-            zs = keep.tile([P, C], U8, name="zs%d" % c, align_bytes=64)
+            n = C - VEC_ABS[c]
             nc.scalar.activation(
-                out=z[:].rearrange("p (u i t) -> p u t i", i=4, t=PACK),
-                in_=diffs[c][:].rearrange("p t (u i) -> p u t i", i=4),
+                out=zs_bf[c][:, : n * PACK].rearrange("p (u i t) -> p u t i", i=4, t=PACK),
+                in_=diffs[c][:, :, :n].rearrange("p t (u i) -> p u t i", i=4),
                 func=ACT.Abs,
             )
-            nc.vector.quantize_mx(out=zc[:].bitcast(FP8X4), scales=zs[:], in_=z[:])
+            if VEC_ABS[c]:
+                part = diffs[c][:, :, n:].rearrange("p t v -> p v t")
+                nc.vector.scalar_tensor_tensor(
+                    out=zs_bf[c][:, n * PACK :].rearrange("p (v t) -> p v t", t=PACK),
+                    in0=part,
+                    scalar=-1.0,
+                    in1=part,
+                    op0=ALU.mult,
+                    op1=ALU.max,
+                )
+        accs = []
+        for c in range(CHUNKS):
+            zc = keep.tile([P, C], U32, name="zc%d" % c, align_bytes=64)
+            zs = keep.tile([P, C], U8, name="zs%d" % c, align_bytes=64)
+            nc.vector.quantize_mx(out=zc[:].bitcast(FP8X4), scales=zs[:], in_=zs_bf[c][:])
             acc = psum.tile([P, C], F32, name="acc%d" % c, tag="b0_%d" % c)
+            accs.append(acc)
             nc.tensor.matmul_mx(
                 out=acc[:],
                 lhsT=w2w[:].bitcast(FP8X4),
@@ -174,6 +192,10 @@ def tile_picked_siam_abs_p_kernel(
                 start=True,
                 stop=True,
             )
+        for c in range(CHUNKS):
             res = keep.tile([P, C], F32, name="res%d" % c)
-            nc.vector.tensor_copy(out=res[:], in_=acc[:])
+            if c == 0:
+                nc.scalar.copy(out=res[:], in_=accs[c][:])
+            else:
+                nc.vector.tensor_copy(out=res[:], in_=accs[c][:])
             nc.sync.dma_start(out=out[:, C * c : C * (c + 1)], in_=res[:])

@@ -20,10 +20,11 @@ PACK = 4
 PASSES = K // (P * PACK)
 C = 128
 CHUNKS = V // C
-VEC_ABS = (0, 64)
-
-FIRST_AT = (0, 128)
-SECOND_AT = (128, 0)
+D = 64
+PIECES = V // D
+HALF = H // 2
+VEC_ABS = (2,)
+OUT_PARTS = ((0, 2), (2, 3), (3, 4))
 
 
 def tile_picked_siam_abs_p_kernel(
@@ -38,13 +39,17 @@ def tile_picked_siam_abs_p_kernel(
         xs = keep.tile([P, T], U8, name="xs", align_bytes=64)
         xw = [keep.tile([P, T], U32, name="xw%d" % g, align_bytes=64) for g in range(PASSES)]
         raw = [keep.tile([P, PACK, H], F32, name="raw%d" % g, align_bytes=64) for g in range(PASSES)]
-        grouped = [
-            [keep.tile([P, H * PACK // 2], BF16, name="grouped%d_%d" % (g, h), align_bytes=64) for h in range(2)]
-            for g in range(PASSES)
+        grouped0 = [keep.tile([P, H * PACK // 2], BF16, name="grouped0_%d" % h, align_bytes=64) for h in range(2)]
+        grouped1 = [
+            [
+                keep.tile([P, H], BF16, name="grouped1_%d_%d" % (a, h), tag="grouped1_%d_%d" % (a, h), align_bytes=64)
+                for h in range(2)
+            ]
+            for a in range(2)
         ]
         w1c = [keep.tile([P, H], U32, name="w1c%d" % g, align_bytes=64) for g in range(PASSES)]
         w1s = [keep.tile([P, H], U8, name="w1s%d" % g, align_bytes=64) for g in range(PASSES)]
-        gw = [keep.tile([P, S], U32, name="gw%d" % g, align_bytes=64) for g in range(PASSES)]
+        gw0 = keep.tile([P, S], U32, name="gw0", align_bytes=64)
         gs = keep.tile([P, S], U8, name="gs", align_bytes=64)
         w2w = keep.tile([P, N], U32, name="w2w", align_bytes=64)
         w2s = keep.tile([P, N], U8, name="w2s", align_bytes=64)
@@ -78,110 +83,117 @@ def tile_picked_siam_abs_p_kernel(
                 in_=w2_scales[0, 4 * q : 4 * q + 4, :].bitcast(I32),
             )
 
-        def gather(dst, window, at, entry, count):
-            nc.vector.tensor_copy(
-                dst[:, at : at + count], window[:].indirect(offsets[:, entry // 16 : (entry + count) // 16])
-            )
-
-        def gather_all(dst, window):
-            gather(dst, window, 0, 0, C)
-            gather(dst, window, C, V, V)
-            gather(dst, window, 3 * C, C, C)
-
-        def interleave(g, h):
-            dst = grouped[g][h][:].rearrange("p (t m j) -> p m t j", t=2, j=PACK)
-            src = raw[g][:].rearrange("p j (m t) -> p m t j", t=PACK)[:, :, 2 * h : 2 * h + 2, :]
+        def interleave(grouped, g, h, rows):
+            dst = grouped[:].rearrange("p (t m j) -> p m t j", t=2, j=PACK)
+            src = raw[g][:].rearrange("p j (m t) -> p j m t", t=PACK)[:, :, rows, 2 * h : 2 * h + 2]
+            src = src.rearrange("p j m t -> p m t j")
             if h == 0:
                 nc.vector.tensor_copy(out=dst, in_=src)
             else:
                 nc.scalar.activation(out=dst, in_=src, func=ACT.Copy)
 
-        def quantize_w1(g, h):
-            cols = slice(h * H // 2, (h + 1) * H // 2)
-            nc.vector.quantize_mx(out=w1c[g][:, cols].bitcast(FP8X4), scales=w1s[g][:, cols], in_=grouped[g][h][:])
+        def quantize_w1(g, first, count, in_):
+            cols = slice(first, first + count)
+            nc.vector.quantize_mx(out=w1c[g][:, cols].bitcast(FP8X4), scales=w1s[g][:, cols], in_=in_)
 
-        banks = [
-            [psum.tile([P, 2 * C], F32, name="h%d_%d" % (c, t), tag="b%d_%d" % (c, t)) for t in range(PACK)]
-            for c in range(CHUNKS)
-        ]
+        def quantize_half(a, h):
+            for i in range(2):
+                t = 2 * h + i
+                quantize_w1(1, P * t + a * P // 2, P // 2, grouped1[a][h][:, i * HALF : (i + 1) * HALF])
 
-        def first_layer(g, c):
-            cols = slice(2 * C * c, 2 * C * (c + 1))
-            for t in range(PACK):
+        banks = [[psum.tile([P, PACK, C], F32, name="h%d_%d" % (c, s), tag="b%d_%d" % (c, s)) for s in range(2)] for c in range(CHUNKS)]
+        words = {}
+
+        def columns(c, s):
+            return slice(V * s + C * c, V * s + C * (c + 1))
+
+        def first_layer(g, c, s, tiles):
+            cols = columns(c, s)
+            for t in tiles:
                 chan = slice(P * t, P * (t + 1))
                 nc.tensor.matmul_mx(
-                    out=banks[c][t][:],
+                    out=banks[c][s][:, t, :],
                     lhsT=w1c[g][:, chan].bitcast(FP8X4),
                     lhsT_scale=w1s[g][:, chan],
-                    rhs=gw[g][:, cols].bitcast(FP8X4),
+                    rhs=words[g, c, s].bitcast(FP8X4),
                     rhs_scale=gs[4 * g : P, cols],
-                    start=(g == 0),
-                    stop=(g == PASSES - 1),
+                    start=(g == 0 and t == 0),
+                    stop=(g == PASSES - 1 and t == PACK - 1),
                 )
 
-        def gather_chunk(c):
-            gather(gw[1], xw[1], 2 * C * c + FIRST_AT[c], C * c, C)
-            gather(gw[1], xw[1], 2 * C * c + SECOND_AT[c], V + C * c, C)
+        def gather_last_pass(dst, c, s):
+            cols = columns(c, s)
+            words[1, c, s] = dst
+            nc.vector.tensor_copy(dst, xw[1][:].indirect(offsets[:, cols.start // 16 : cols.stop // 16]))
 
-        gather_all(gw[0], xw[0])
-        gather_all(gs, xs)
-        interleave(0, 0)
-        interleave(0, 1)
-        quantize_w1(0, 0)
-        quantize_w1(0, 1)
-        for c in range(CHUNKS):
-            first_layer(0, c)
-        interleave(1, 0)
-        interleave(1, 1)
-        quantize_w1(1, 0)
-        gather_chunk(0)
-        quantize_w1(1, 1)
-        gather_chunk(1)
-        for c in range(CHUNKS):
-            first_layer(1, c)
+        order = [(c, s) for c in range(CHUNKS) for s in (1, 0)]
+        nc.vector.tensor_copy(gw0[:], xw[0][:].indirect(offsets[:]))
+        for c, s in order:
+            words[0, c, s] = gw0[:, columns(c, s)]
+        nc.vector.tensor_copy(gs[:], xs[:].indirect(offsets[:]))
+        for h in range(2):
+            interleave(grouped0[h], 0, h, slice(0, P))
+        for h in range(2):
+            quantize_w1(0, h * HALF, HALF, grouped0[h][:])
+            for c, s in order:
+                first_layer(0, c, s, (2 * h, 2 * h + 1))
+        for a in range(2):
+            for h in range(2):
+                interleave(grouped1[a][h], 1, h, slice(a * P // 2, (a + 1) * P // 2))
+        quantize_half(0, 0)
+        quantize_half(0, 1)
+        quantize_half(1, 0)
+        lead = keep.tile([P, C], U32, name="lead", align_bytes=64)
+        gather_last_pass(lead[:], *order[0])
+        quantize_half(1, 1)
+        first_layer(1, *order[0], range(PACK))
+        rest = keep.tile([P, S - C], U32, name="rest", tag="grouped1_1_1", align_bytes=64)
+        for i, (c, s) in enumerate(order[1:]):
+            gather_last_pass(rest[:, C * i : C * (i + 1)], c, s)
+            first_layer(1, c, s, range(PACK))
+
+        def view(ap):
+            return ap.rearrange("p (v t) -> p v t", t=PACK)
 
         diffs = []
-        for c in range(CHUNKS):
-            second = keep.tile([P, PACK, C], F32, name="second%d" % c)
-            diff = keep.tile([P, PACK, C], F32, name="diff%d" % c)
+        seconds = []
+        for i in range(PIECES):
+            c, at = divmod(i * D, C)
+            second = keep.tile([P, D * PACK], F32, name="second%d" % i)
+            diff = keep.tile([P, D * PACK], BF16, name="diff%d" % i)
             diffs.append(diff)
-            for t in range(PACK):
-                bank = banks[c][t]
-                nc.scalar.activation(
-                    out=second[:, t, :], in_=bank[:, SECOND_AT[c] : SECOND_AT[c] + C], func=ACT.Relu
-                )
-                nc.vector.scalar_tensor_tensor(
-                    out=diff[:, t, :],
-                    in0=bank[:, FIRST_AT[c] : FIRST_AT[c] + C],
-                    scalar=0.0,
-                    in1=second[:, t, :],
-                    op0=ALU.max,
-                    op1=ALU.subtract,
-                )
-        zs_bf = [keep.tile([P, C * PACK], BF16, name="z%d" % c, align_bytes=64) for c in range(CHUNKS)]
-        for c in range(CHUNKS):
-            n = C - VEC_ABS[c]
+            seconds.append(second)
             nc.scalar.activation(
-                out=zs_bf[c][:, : n * PACK].rearrange("p (u i t) -> p u t i", i=4, t=PACK),
-                in_=diffs[c][:, :, :n].rearrange("p t (u i) -> p u t i", i=4),
-                func=ACT.Abs,
+                out=view(second[:]), in_=banks[c][1][:, :, at : at + D].rearrange("p t v -> p v t"), func=ACT.Relu
             )
-            if VEC_ABS[c]:
-                part = diffs[c][:, :, n:].rearrange("p t v -> p v t")
-                nc.vector.scalar_tensor_tensor(
-                    out=zs_bf[c][:, n * PACK :].rearrange("p (v t) -> p v t", t=PACK),
-                    in0=part,
-                    scalar=-1.0,
-                    in1=part,
-                    op0=ALU.mult,
-                    op1=ALU.max,
-                )
+            nc.vector.scalar_tensor_tensor(
+                out=view(diff[:]),
+                in0=banks[c][0][:, :, at : at + D].rearrange("p t v -> p v t"),
+                scalar=0.0,
+                in1=view(second[:]),
+                op0=ALU.max,
+                op1=ALU.subtract,
+            )
+        z = []
+        for k, (lo, hi) in enumerate(OUT_PARTS):
+            z.append(keep.tile([P, (hi - lo) * D * PACK], BF16, name="z%d" % k, align_bytes=64))
+            for i in range(lo, hi):
+                dst = z[k][:, (i - lo) * D * PACK : (i - lo + 1) * D * PACK]
+                if i in VEC_ABS:
+                    nc.vector.scalar_tensor_tensor(
+                        out=dst, in0=diffs[i][:], scalar=-1.0, in1=diffs[i][:], op0=ALU.mult, op1=ALU.max
+                    )
+                else:
+                    nc.scalar.activation(out=dst, in_=diffs[i][:], func=ACT.Abs)
         accs = []
-        for c in range(CHUNKS):
-            zc = keep.tile([P, C], U32, name="zc%d" % c, align_bytes=64)
-            zs = keep.tile([P, C], U8, name="zs%d" % c, align_bytes=64)
-            nc.vector.quantize_mx(out=zc[:].bitcast(FP8X4), scales=zs[:], in_=zs_bf[c][:])
-            acc = psum.tile([P, C], F32, name="acc%d" % c, tag="b0_%d" % c)
+        zcs = []
+        for k, (lo, hi) in enumerate(OUT_PARTS):
+            n = (hi - lo) * D
+            zc = keep.tile([P, n], U32, name="zc%d" % k, align_bytes=64)
+            zs = keep.tile([P, n], U8, name="zs%d" % k, align_bytes=64)
+            zcs.append(zc)
+            nc.vector.quantize_mx(out=zc[:].bitcast(FP8X4), scales=zs[:], in_=z[k][:])
+            acc = psum.tile([P, n], F32, name="acc%d" % k, tag="acc%d" % k)
             accs.append(acc)
             nc.tensor.matmul_mx(
                 out=acc[:],
@@ -192,10 +204,13 @@ def tile_picked_siam_abs_p_kernel(
                 start=True,
                 stop=True,
             )
-        for c in range(CHUNKS):
-            res = keep.tile([P, C], F32, name="res%d" % c)
-            if c == 0:
-                nc.scalar.copy(out=res[:], in_=accs[c][:])
+        res = [keep.tile([P, C], F32, name="res%d" % c) for c in range(CHUNKS)]
+        for k, (lo, hi) in enumerate(OUT_PARTS):
+            c, at = divmod(lo * D, C)
+            dst = res[c][:, at : at + (hi - lo) * D]
+            if k < len(OUT_PARTS) - 1:
+                nc.scalar.copy(out=dst, in_=accs[k][:])
             else:
-                nc.vector.tensor_copy(out=res[:], in_=accs[c][:])
-            nc.sync.dma_start(out=out[:, C * c : C * (c + 1)], in_=res[:])
+                nc.vector.tensor_copy(out=dst, in_=accs[k][:])
+            if (hi * D) % C == 0:
+                nc.sync.dma_start(out=out[:, C * c : C * (c + 1)], in_=res[c][:])

@@ -38,7 +38,7 @@ def tile_picked_siam_abs_p_kernel(
         offsets = keep.tile([P, S // 16], U16, name="offsets")
         xs = keep.tile([P, T], U8, name="xs", align_bytes=64)
         xw = [keep.tile([P, T], U32, name="xw%d" % g, align_bytes=64) for g in range(PASSES)]
-        raw = [keep.tile([P, PACK, H], F32, name="raw%d" % g, align_bytes=64) for g in range(PASSES)]
+        raw = [keep.tile([P, PACK, H], F32, name="raw%d" % g, tag="raw%d" % g, align_bytes=64) for g in range(PASSES)]
         grouped0 = [keep.tile([P, H * PACK // 2], BF16, name="grouped0_%d" % h, align_bytes=64) for h in range(2)]
         grouped1 = [
             [
@@ -84,9 +84,9 @@ def tile_picked_siam_abs_p_kernel(
             )
 
         def interleave(grouped, g, h, rows):
-            dst = grouped[:].rearrange("p (t m j) -> p m t j", t=2, j=PACK)
+            dst = grouped[:].rearrange("p (t m j) -> p m j t", t=2, j=PACK)
             src = raw[g][:].rearrange("p j (m t) -> p j m t", t=PACK)[:, :, rows, 2 * h : 2 * h + 2]
-            src = src.rearrange("p j m t -> p m t j")
+            src = src.rearrange("p j m t -> p m j t")
             if h == 0:
                 nc.vector.tensor_copy(out=dst, in_=src)
             else:
@@ -143,13 +143,10 @@ def tile_picked_siam_abs_p_kernel(
         quantize_half(0, 0)
         quantize_half(0, 1)
         quantize_half(1, 0)
-        lead = keep.tile([P, C], U32, name="lead", align_bytes=64)
-        gather_last_pass(lead[:], *order[0])
         quantize_half(1, 1)
-        first_layer(1, *order[0], range(PACK))
-        rest = keep.tile([P, S - C], U32, name="rest", tag="grouped1_1_1", align_bytes=64)
-        for i, (c, s) in enumerate(order[1:]):
-            gather_last_pass(rest[:, C * i : C * (i + 1)], c, s)
+        gw1 = keep.tile([P, S], U32, name="gw1", tag="raw1", align_bytes=64)
+        for c, s in order:
+            gather_last_pass(gw1[:, columns(c, s)], c, s)
             first_layer(1, c, s, range(PACK))
 
         def view(ap):

@@ -64,8 +64,8 @@ def tile_picked_siam_abs_p_kernel(
 
         nc.gpsimd.memset(xs[:].bitcast(I32), 0)
         nc.gpsimd.memset(w2s[:].bitcast(I32), 0)
-        nc.sync.dma_start(offsets[:], offs)
         load_x(0)
+        nc.sync.dma_start(offsets[:], offs)
         for q in range(4):
             nc.sync.dma_start(
                 out=xs[32 * q : 32 * q + 4 * PASSES, :].bitcast(I32),
@@ -143,10 +143,13 @@ def tile_picked_siam_abs_p_kernel(
         quantize_half(0, 0)
         quantize_half(0, 1)
         quantize_half(1, 0)
+        lead = keep.tile([P, C], U32, name="lead", align_bytes=64)
+        gather_last_pass(lead[:], *order[0])
         quantize_half(1, 1)
-        gw1 = keep.tile([P, S], U32, name="gw1", tag="raw1", align_bytes=64)
-        for c, s in order:
-            gather_last_pass(gw1[:, columns(c, s)], c, s)
+        first_layer(1, *order[0], range(PACK))
+        rest = keep.tile([P, S - C], U32, name="rest", tag="raw1", align_bytes=64)
+        for i, (c, s) in enumerate(order[1:]):
+            gather_last_pass(rest[:, C * i : C * (i + 1)], c, s)
             first_layer(1, c, s, range(PACK))
 
         def view(ap):

@@ -40,13 +40,8 @@ def tile_picked_siam_abs_p_kernel(
         xw = [keep.tile([P, T], U32, name="xw%d" % g, align_bytes=64) for g in range(PASSES)]
         raw = [keep.tile([P, PACK, H], F32, name="raw%d" % g, tag="raw%d" % g, align_bytes=64) for g in range(PASSES)]
         grouped0 = [keep.tile([P, H * PACK // 2], BF16, name="grouped0_%d" % h, align_bytes=64) for h in range(2)]
-        grouped1 = [
-            [
-                keep.tile([P, H], BF16, name="grouped1_%d_%d" % (a, h), tag="grouped1_%d_%d" % (a, h), align_bytes=64)
-                for h in range(2)
-            ]
-            for a in range(2)
-        ]
+        grouped1 = keep.tile([P, H * PACK // 2], BF16, name="grouped1", align_bytes=64)
+        halves1 = [keep.tile([P, H], BF16, name="halves1_%d" % a, align_bytes=64) for a in range(2)]
         w1c = [keep.tile([P, H], U32, name="w1c%d" % g, align_bytes=64) for g in range(PASSES)]
         w1s = [keep.tile([P, H], U8, name="w1s%d" % g, align_bytes=64) for g in range(PASSES)]
         gw0 = keep.tile([P, S], U32, name="gw0", align_bytes=64)
@@ -96,10 +91,9 @@ def tile_picked_siam_abs_p_kernel(
             cols = slice(first, first + count)
             nc.vector.quantize_mx(out=w1c[g][:, cols].bitcast(FP8X4), scales=w1s[g][:, cols], in_=in_)
 
-        def quantize_half(a, h):
+        def quantize_half(a):
             for i in range(2):
-                t = 2 * h + i
-                quantize_w1(1, P * t + a * P // 2, P // 2, grouped1[a][h][:, i * HALF : (i + 1) * HALF])
+                quantize_w1(1, P * (2 + i) + a * P // 2, P // 2, halves1[a][:, i * HALF : (i + 1) * HALF])
 
         banks = [[psum.tile([P, PACK, C], F32, name="h%d_%d" % (c, s), tag="b%d_%d" % (c, s)) for s in range(2)] for c in range(CHUNKS)]
         words = {}
@@ -137,15 +131,14 @@ def tile_picked_siam_abs_p_kernel(
             quantize_w1(0, h * HALF, HALF, grouped0[h][:])
             for c, s in order:
                 first_layer(0, c, s, (2 * h, 2 * h + 1))
+        interleave(grouped1, 1, 0, slice(0, P))
         for a in range(2):
-            for h in range(2):
-                interleave(grouped1[a][h], 1, h, slice(a * P // 2, (a + 1) * P // 2))
-        quantize_half(0, 0)
-        quantize_half(0, 1)
-        quantize_half(1, 0)
+            interleave(halves1[a], 1, 1, slice(a * P // 2, (a + 1) * P // 2))
+        quantize_half(0)
+        quantize_w1(1, 0, HALF, grouped1[:])
         lead = keep.tile([P, C], U32, name="lead", align_bytes=64)
         gather_last_pass(lead[:], *order[0])
-        quantize_half(1, 1)
+        quantize_half(1)
         first_layer(1, *order[0], range(PACK))
         rest = keep.tile([P, S - C], U32, name="rest", tag="raw1", align_bytes=64)
         for i, (c, s) in enumerate(order[1:]):

@@ -37,11 +37,10 @@ def tile_picked_siam_abs_p_kernel(
 
         offsets = keep.tile([P, S // 16], U16, name="offsets")
         xs = keep.tile([P, T], U8, name="xs", align_bytes=64)
-        xw = [keep.tile([P, T], U32, name="xw%d" % g, align_bytes=64) for g in range(PASSES)]
+        xw = [keep.tile([P, T], U32, name="xw%d" % g, tag="xw%d" % g, align_bytes=64) for g in range(PASSES)]
         raw = [keep.tile([P, PACK, H], F32, name="raw%d" % g, tag="raw%d" % g, align_bytes=64) for g in range(PASSES)]
         grouped0 = [keep.tile([P, H * PACK // 2], BF16, name="grouped0_%d" % h, align_bytes=64) for h in range(2)]
-        grouped1 = keep.tile([P, H * PACK // 2], BF16, name="grouped1", align_bytes=64)
-        halves1 = [keep.tile([P, H], BF16, name="halves1_%d" % a, align_bytes=64) for a in range(2)]
+        grouped1 = [keep.tile([P, H * PACK // 2], BF16, name="grouped1_%d" % h, align_bytes=64) for h in range(2)]
         w1c = [keep.tile([P, H], U32, name="w1c%d" % g, align_bytes=64) for g in range(PASSES)]
         w1s = [keep.tile([P, H], U8, name="w1s%d" % g, align_bytes=64) for g in range(PASSES)]
         gw0 = keep.tile([P, S], U32, name="gw0", align_bytes=64)
@@ -91,10 +90,6 @@ def tile_picked_siam_abs_p_kernel(
             cols = slice(first, first + count)
             nc.vector.quantize_mx(out=w1c[g][:, cols].bitcast(FP8X4), scales=w1s[g][:, cols], in_=in_)
 
-        def quantize_half(a):
-            for i in range(2):
-                quantize_w1(1, P * (2 + i) + a * P // 2, P // 2, halves1[a][:, i * HALF : (i + 1) * HALF])
-
         banks = [[psum.tile([P, PACK, C], F32, name="h%d_%d" % (c, s), tag="b%d_%d" % (c, s)) for s in range(2)] for c in range(CHUNKS)]
         words = {}
 
@@ -127,23 +122,28 @@ def tile_picked_siam_abs_p_kernel(
         nc.vector.tensor_copy(gs[:], xs[:].indirect(offsets[:]))
         for h in range(2):
             interleave(grouped0[h], 0, h, slice(0, P))
-        for h in range(2):
-            quantize_w1(0, h * HALF, HALF, grouped0[h][:])
+        for t in range(2):
+            quantize_w1(0, t * P, P, grouped0[0][:, t * H : (t + 1) * H])
             for c, s in order:
-                first_layer(0, c, s, (2 * h, 2 * h + 1))
-        interleave(grouped1, 1, 0, slice(0, P))
-        for a in range(2):
-            interleave(halves1[a], 1, 1, slice(a * P // 2, (a + 1) * P // 2))
-        quantize_half(0)
-        quantize_w1(1, 0, HALF, grouped1[:])
+                first_layer(0, c, s, (t,))
+        quantize_w1(0, HALF, HALF, grouped0[1][:])
+        for c, s in order:
+            first_layer(0, c, s, (2, 3))
+        for h in range(2):
+            interleave(grouped1[h], 1, h, slice(0, P))
+        quantize_w1(1, 0, HALF, grouped1[0][:])
         lead = keep.tile([P, C], U32, name="lead", align_bytes=64)
         gather_last_pass(lead[:], *order[0])
-        quantize_half(1)
+        quantize_w1(1, HALF, HALF, grouped1[1][:])
         first_layer(1, *order[0], range(PACK))
         rest = keep.tile([P, S - C], U32, name="rest", tag="raw1", align_bytes=64)
         for i, (c, s) in enumerate(order[1:]):
             gather_last_pass(rest[:, C * i : C * (i + 1)], c, s)
             first_layer(1, c, s, range(PACK))
+
+        w2 = keep.tile([P, N + N // PACK], I32, name="w2", tag="xw1", align_bytes=64)
+        nc.gpsimd.tensor_copy(out=w2[:, :N], in_=w2w[:].bitcast(I32))
+        nc.gpsimd.tensor_copy(out=w2[:, N:], in_=w2s[:].bitcast(I32))
 
         def view(ap):
             return ap.rearrange("p (v t) -> p v t", t=PACK)
@@ -190,8 +190,8 @@ def tile_picked_siam_abs_p_kernel(
             accs.append(acc)
             nc.tensor.matmul_mx(
                 out=acc[:],
-                lhsT=w2w[:].bitcast(FP8X4),
-                lhsT_scale=w2s[:],
+                lhsT=w2[:, :N].bitcast(FP8X4),
+                lhsT_scale=w2[:, N:].bitcast(U8),
                 rhs=zc[:].bitcast(FP8X4),
                 rhs_scale=zs[:],
                 start=True,

@@ -45,7 +45,6 @@ def tile_picked_siam_abs_p_kernel(
         w1s = [keep.tile([P, H], U8, name="w1s%d" % g, align_bytes=64) for g in range(PASSES)]
         gw0 = keep.tile([P, S], U32, name="gw0", align_bytes=64)
         gs = keep.tile([P, S], U8, name="gs", align_bytes=64)
-        w2w = keep.tile([P, N], U32, name="w2w", align_bytes=64)
         w2s = keep.tile([P, N], U8, name="w2s", align_bytes=64)
 
         def load_w1(g):
@@ -65,17 +64,18 @@ def tile_picked_siam_abs_p_kernel(
                 out=xs[32 * q : 32 * q + 4 * PASSES, :].bitcast(I32),
                 in_=x_scales[:, 4 * q : 4 * q + 4, :].bitcast(I32),
             )
+
+        def load_w2_scales(quadrants):
+            for q in quadrants:
+                nc.sync.dma_start(
+                    out=w2s[32 * q : 32 * q + 4, :].bitcast(I32),
+                    in_=w2_scales[0, 4 * q : 4 * q + 4, :].bitcast(I32),
+                )
+
+        load_w2_scales(range(1))
         load_w1(0)
         load_w1(1)
         load_x(1)
-        nc.sync.dma_start(
-            out=w2w[:].bitcast(I32), in_=w2_words[0].rearrange("p n t -> p (n t)").bitcast(I32)
-        )
-        for q in range(4):
-            nc.sync.dma_start(
-                out=w2s[32 * q : 32 * q + 4, :].bitcast(I32),
-                in_=w2_scales[0, 4 * q : 4 * q + 4, :].bitcast(I32),
-            )
 
         def interleave(grouped, g, h, rows):
             dst = grouped[:].rearrange("p (t m j) -> p m j t", t=2, j=PACK)
@@ -122,6 +122,11 @@ def tile_picked_siam_abs_p_kernel(
         nc.vector.tensor_copy(gs[:], xs[:].indirect(offsets[:]))
         for h in range(2):
             interleave(grouped0[h], 0, h, slice(0, P))
+        w2w = keep.tile([P, N], U32, name="w2w", tag="raw0", align_bytes=64)
+        nc.sync.dma_start(
+            out=w2w[:].bitcast(I32), in_=w2_words[0].rearrange("p n t -> p (n t)").bitcast(I32)
+        )
+        load_w2_scales(range(1, 4))
         for t in range(2):
             quantize_w1(0, t * P, P, grouped0[0][:, t * H : (t + 1) * H])
             for c, s in order:
@@ -201,7 +206,7 @@ def tile_picked_siam_abs_p_kernel(
         for k, (lo, hi) in enumerate(OUT_PARTS):
             c, at = divmod(lo * D, C)
             dst = res[c][:, at : at + (hi - lo) * D]
-            if k < len(OUT_PARTS) - 1:
+            if c == 0:
                 nc.scalar.copy(out=dst, in_=accs[k][:])
             else:
                 nc.vector.tensor_copy(out=dst, in_=accs[k][:])

@@ -20,11 +20,10 @@ PACK = 4
 PASSES = K // (P * PACK)
 C = 128
 CHUNKS = V // C
-D = 64
-PIECES = V // D
 HALF = H // 2
-VEC_ABS = (2,)
-OUT_PARTS = ((0, 2), (2, 3), (3, 4))
+SHARE1 = 84
+TILES = (2, 4)
+PARTS = ((0, 128), (128, 64), (192, 64))
 
 
 def tile_picked_siam_abs_p_kernel(
@@ -39,8 +38,10 @@ def tile_picked_siam_abs_p_kernel(
         xs = keep.tile([P, T], U8, name="xs", align_bytes=64)
         xw = [keep.tile([P, T], U32, name="xw%d" % g, tag="xw%d" % g, align_bytes=64) for g in range(PASSES)]
         raw = [keep.tile([P, PACK, H], F32, name="raw%d" % g, tag="raw%d" % g, align_bytes=64) for g in range(PASSES)]
-        grouped0 = [keep.tile([P, H * PACK // 2], BF16, name="grouped0_%d" % h, align_bytes=64) for h in range(2)]
-        grouped1 = [keep.tile([P, H * PACK // 2], BF16, name="grouped1_%d" % h, align_bytes=64) for h in range(2)]
+        grouped = [
+            [keep.tile([P, H * 2], BF16, name="grouped%d_%d" % (g, h), align_bytes=64) for h in range(2)]
+            for g in range(PASSES)
+        ]
         w1c = [keep.tile([P, H], U32, name="w1c%d" % g, align_bytes=64) for g in range(PASSES)]
         w1s = [keep.tile([P, H], U8, name="w1s%d" % g, align_bytes=64) for g in range(PASSES)]
         gw0 = keep.tile([P, S], U32, name="gw0", align_bytes=64)
@@ -55,6 +56,13 @@ def tile_picked_siam_abs_p_kernel(
             src = x_words[g].rearrange("p n t -> p (n t)").bitcast(I32)
             nc.sync.dma_start(out=xw[g][:].bitcast(I32), in_=src)
 
+        def load_w2_scales(quadrants):
+            for q in quadrants:
+                nc.sync.dma_start(
+                    out=w2s[32 * q : 32 * q + 4, :].bitcast(I32),
+                    in_=w2_scales[0, 4 * q : 4 * q + 4, :].bitcast(I32),
+                )
+
         nc.gpsimd.memset(xs[:].bitcast(I32), 0)
         nc.gpsimd.memset(w2s[:].bitcast(I32), 0)
         load_x(0)
@@ -64,24 +72,15 @@ def tile_picked_siam_abs_p_kernel(
                 out=xs[32 * q : 32 * q + 4 * PASSES, :].bitcast(I32),
                 in_=x_scales[:, 4 * q : 4 * q + 4, :].bitcast(I32),
             )
-
-        def load_w2_scales(quadrants):
-            for q in quadrants:
-                nc.sync.dma_start(
-                    out=w2s[32 * q : 32 * q + 4, :].bitcast(I32),
-                    in_=w2_scales[0, 4 * q : 4 * q + 4, :].bitcast(I32),
-                )
-
         load_w2_scales(range(1))
         load_w1(0)
         load_w1(1)
         load_x(1)
 
-        def interleave(grouped, g, h, rows):
-            dst = grouped[:].rearrange("p (t m j) -> p m j t", t=2, j=PACK)
-            src = raw[g][:].rearrange("p j (m t) -> p j m t", t=PACK)[:, :, rows, 2 * h : 2 * h + 2]
-            src = src.rearrange("p j m t -> p m j t")
-            if h == 0:
+        def interleave(g, h, cols, on_vector):
+            dst = grouped[g][h][:].rearrange("p (t m j) -> p m j t", t=2, j=PACK)[:, cols]
+            src = raw[g][:].rearrange("p j (m t) -> p m j t", t=PACK)[:, cols, :, 2 * h : 2 * h + 2]
+            if on_vector:
                 nc.vector.tensor_copy(out=dst, in_=src)
             else:
                 nc.scalar.activation(out=dst, in_=src, func=ACT.Copy)
@@ -90,25 +89,28 @@ def tile_picked_siam_abs_p_kernel(
             cols = slice(first, first + count)
             nc.vector.quantize_mx(out=w1c[g][:, cols].bitcast(FP8X4), scales=w1s[g][:, cols], in_=in_)
 
-        banks = [[psum.tile([P, PACK, C], F32, name="h%d_%d" % (c, s), tag="b%d_%d" % (c, s)) for s in range(2)] for c in range(CHUNKS)]
+        banks = {
+            (c, s, h): psum.tile([P, TILES[c], C], F32, name="h%d_%d_%d" % (c, s, h), tag="b%d_%d_%d" % (c, s, h))
+            for c in range(CHUNKS)
+            for s in range(2)
+            for h in range(PACK // TILES[c])
+        }
         words = {}
 
         def columns(c, s):
             return slice(V * s + C * c, V * s + C * (c + 1))
 
-        def first_layer(g, c, s, tiles):
-            cols = columns(c, s)
-            for t in tiles:
-                chan = slice(P * t, P * (t + 1))
-                nc.tensor.matmul_mx(
-                    out=banks[c][s][:, t, :],
-                    lhsT=w1c[g][:, chan].bitcast(FP8X4),
-                    lhsT_scale=w1s[g][:, chan],
-                    rhs=words[g, c, s].bitcast(FP8X4),
-                    rhs_scale=gs[4 * g : P, cols],
-                    start=(g == 0 and t == 0),
-                    stop=(g == PASSES - 1 and t == PACK - 1),
-                )
+        def product(g, c, s, t):
+            chan = slice(P * t, P * (t + 1))
+            nc.tensor.matmul_mx(
+                out=banks[c, s, t // TILES[c]][:, t % TILES[c], :],
+                lhsT=w1c[g][:, chan].bitcast(FP8X4),
+                lhsT_scale=w1s[g][:, chan],
+                rhs=words[g, c, s].bitcast(FP8X4),
+                rhs_scale=gs[4 * g : P, columns(c, s)],
+                start=(g == 0 and t % TILES[c] == 0),
+                stop=(g == PASSES - 1 and t % TILES[c] == TILES[c] - 1),
+            )
 
         def gather_last_pass(dst, c, s):
             cols = columns(c, s)
@@ -121,77 +123,102 @@ def tile_picked_siam_abs_p_kernel(
             words[0, c, s] = gw0[:, columns(c, s)]
         nc.vector.tensor_copy(gs[:], xs[:].indirect(offsets[:]))
         for h in range(2):
-            interleave(grouped0[h], 0, h, slice(0, P))
+            interleave(0, h, slice(0, P), h == 0)
         w2w = keep.tile([P, N], U32, name="w2w", tag="raw0", align_bytes=64)
-        nc.sync.dma_start(
-            out=w2w[:].bitcast(I32), in_=w2_words[0].rearrange("p n t -> p (n t)").bitcast(I32)
-        )
+        nc.sync.dma_start(out=w2w[:].bitcast(I32), in_=w2_words[0].rearrange("p n t -> p (n t)").bitcast(I32))
         load_w2_scales(range(1, 4))
         for t in range(2):
-            quantize_w1(0, t * P, P, grouped0[0][:, t * H : (t + 1) * H])
+            quantize_w1(0, t * P, P, grouped[0][0][:, t * H : (t + 1) * H])
             for c, s in order:
-                first_layer(0, c, s, (t,))
-        quantize_w1(0, HALF, HALF, grouped0[1][:])
+                product(0, c, s, t)
+        quantize_w1(0, HALF, HALF, grouped[0][1][:])
         for c, s in order:
-            first_layer(0, c, s, (2, 3))
-        for h in range(2):
-            interleave(grouped1[h], 1, h, slice(0, P))
-        quantize_w1(1, 0, HALF, grouped1[0][:])
-        lead = keep.tile([P, C], U32, name="lead", align_bytes=64)
-        gather_last_pass(lead[:], *order[0])
-        quantize_w1(1, HALF, HALF, grouped1[1][:])
-        first_layer(1, *order[0], range(PACK))
-        rest = keep.tile([P, S - C], U32, name="rest", tag="raw1", align_bytes=64)
-        for i, (c, s) in enumerate(order[1:]):
+            for t in (2, 3):
+                product(0, c, s, t)
+
+        interleave(1, 0, slice(0, SHARE1), True)
+        interleave(1, 0, slice(SHARE1, P), False)
+        interleave(1, 1, slice(0, P), False)
+        quantize_w1(1, 0, HALF, grouped[1][0][:])
+        lead = keep.tile([P, 2 * C], U32, name="lead", align_bytes=64)
+        for i, (c, s) in enumerate(order[:2]):
+            gather_last_pass(lead[:, C * i : C * (i + 1)], c, s)
+            for t in (0, 1):
+                product(1, c, s, t)
+        quantize_w1(1, HALF, HALF, grouped[1][1][:])
+        for c, s in order[:2]:
+            for t in (2, 3):
+                product(1, c, s, t)
+        rest = keep.tile([P, S - 2 * C], U32, name="rest", tag="raw1", align_bytes=64)
+        for i, (c, s) in enumerate(order[2:]):
             gather_last_pass(rest[:, C * i : C * (i + 1)], c, s)
-            first_layer(1, c, s, range(PACK))
+            for t in range(PACK):
+                product(1, c, s, t)
 
         w2 = keep.tile([P, N + N // PACK], I32, name="w2", tag="xw1", align_bytes=64)
         nc.gpsimd.tensor_copy(out=w2[:, :N], in_=w2w[:].bitcast(I32))
         nc.gpsimd.tensor_copy(out=w2[:, N:], in_=w2s[:].bitcast(I32))
 
-        def view(ap):
-            return ap.rearrange("p (v t) -> p v t", t=PACK)
+        diffs = [keep.tile([P, PACK // TILES[c], C, TILES[c]], BF16, name="diff%d" % c) for c in range(CHUNKS)]
+        z = [keep.tile([P, n * PACK], BF16, name="z%d" % k, align_bytes=64) for k, (first, n) in enumerate(PARTS)]
 
-        diffs = []
-        seconds = []
-        for i in range(PIECES):
-            c, at = divmod(i * D, C)
-            second = keep.tile([P, D * PACK], F32, name="second%d" % i)
-            diff = keep.tile([P, D * PACK], BF16, name="diff%d" % i)
-            diffs.append(diff)
-            seconds.append(second)
-            nc.scalar.activation(
-                out=view(second[:]), in_=banks[c][1][:, :, at : at + D].rearrange("p t v -> p v t"), func=ACT.Relu
-            )
+        seconds = {
+            (c, h): keep.tile([P, C, TILES[c]], F32, name="second%d_%d" % (c, h))
+            for c in range(CHUNKS)
+            for h in range(PACK // TILES[c])
+        }
+
+        def relu(c, h, at, n, on_vector):
+            src = banks[c, 1, h][:, :, at : at + n].rearrange("p e v -> p v e")
+            if on_vector:
+                nc.vector.tensor_scalar_max(seconds[c, h][:, at : at + n, :], src, 0.0)
+            else:
+                nc.scalar.activation(out=seconds[c, h][:, at : at + n, :], in_=src, func=ACT.Relu)
+
+        def difference(c, h, at, n):
             nc.vector.scalar_tensor_tensor(
-                out=view(diff[:]),
-                in0=banks[c][0][:, :, at : at + D].rearrange("p t v -> p v t"),
+                out=diffs[c][:, h, at : at + n, :],
+                in0=banks[c, 0, h][:, :, at : at + n].rearrange("p e v -> p v e"),
                 scalar=0.0,
-                in1=view(second[:]),
+                in1=seconds[c, h][:, at : at + n, :],
                 op0=ALU.max,
                 op1=ALU.subtract,
             )
-        z = []
-        for k, (lo, hi) in enumerate(OUT_PARTS):
-            z.append(keep.tile([P, (hi - lo) * D * PACK], BF16, name="z%d" % k, align_bytes=64))
-            for i in range(lo, hi):
-                dst = z[k][:, (i - lo) * D * PACK : (i - lo + 1) * D * PACK]
-                if i in VEC_ABS:
-                    nc.vector.scalar_tensor_tensor(
-                        out=dst, in0=diffs[i][:], scalar=-1.0, in1=diffs[i][:], op0=ALU.mult, op1=ALU.max
-                    )
-                else:
-                    nc.scalar.activation(out=dst, in_=diffs[i][:], func=ACT.Abs)
+
+        def absolute(c, at, n, on_vector=False):
+            first = c * C + at
+            k = max(i for i, (lo, count) in enumerate(PARTS) if lo <= first)
+            first = first - PARTS[k][0]
+            dst = z[k][:, first * PACK : (first + n) * PACK]
+            if on_vector:
+                src = diffs[c][:, 0, at : at + n, :].rearrange("p v e -> p (v e)")
+                nc.vector.scalar_tensor_tensor(out=dst, in0=src, scalar=-1.0, in1=src, op0=ALU.mult, op1=ALU.max)
+            else:
+                nc.scalar.activation(
+                    out=dst.rearrange("p (v h e) -> p v h e", h=PACK // TILES[c], e=TILES[c]),
+                    in_=diffs[c][:, :, at : at + n, :].rearrange("p h v e -> p v h e"),
+                    func=ACT.Abs,
+                )
+
+        relu(0, 0, 0, 128, False)
+        difference(0, 0, 0, 128)
+        relu(0, 1, 0, 128, False)
+        difference(0, 1, 0, 128)
+        for at in range(0, 128, 32):
+            relu(1, 0, at, 32, False)
+            difference(1, 0, at, 32)
+        absolute(0, 0, 128)
+        absolute(1, 0, 64, True)
+        absolute(1, 64, 32)
+        absolute(1, 96, 32)
+
+        res = [keep.tile([P, C], F32, name="res%d" % c) for c in range(CHUNKS)]
         accs = []
-        zcs = []
-        for k, (lo, hi) in enumerate(OUT_PARTS):
-            n = (hi - lo) * D
+        for k, (first, n) in enumerate(PARTS):
             zc = keep.tile([P, n], U32, name="zc%d" % k, align_bytes=64)
             zs = keep.tile([P, n], U8, name="zs%d" % k, align_bytes=64)
-            zcs.append(zc)
             nc.vector.quantize_mx(out=zc[:].bitcast(FP8X4), scales=zs[:], in_=z[k][:])
-            acc = psum.tile([P, n], F32, name="acc%d" % k, tag="acc%d" % k)
+            acc = psum.tile([P, n], F32, name="acc%d" % k, tag=("b0_1_0", "b0_1_1", "b0_0_0")[k])
             accs.append(acc)
             nc.tensor.matmul_mx(
                 out=acc[:],
@@ -202,13 +229,11 @@ def tile_picked_siam_abs_p_kernel(
                 start=True,
                 stop=True,
             )
-        res = [keep.tile([P, C], F32, name="res%d" % c) for c in range(CHUNKS)]
-        for k, (lo, hi) in enumerate(OUT_PARTS):
-            c, at = divmod(lo * D, C)
-            dst = res[c][:, at : at + (hi - lo) * D]
+        for k, (first, n) in enumerate(PARTS):
+            c, at = divmod(first, C)
             if c == 0:
-                nc.scalar.copy(out=dst, in_=accs[k][:])
+                nc.scalar.copy(out=res[c][:, at : at + n], in_=accs[k][:])
             else:
-                nc.vector.tensor_copy(out=dst, in_=accs[k][:])
-            if (hi * D) % C == 0:
+                nc.vector.tensor_copy(out=res[c][:, at : at + n], in_=accs[k][:])
+            if (first + n) % C == 0:
                 nc.sync.dma_start(out=out[:, C * c : C * (c + 1)], in_=res[c][:])

@@ -21,7 +21,8 @@ PASSES = K // (P * PACK)
 C = 128
 CHUNKS = V // C
 HALF = H // 2
-SHARE1 = 84
+SHARE0 = 84
+SHARE1 = 104
 TILES = (2, 4)
 PARTS = ((0, 128), (128, 64), (192, 64))
 
@@ -32,15 +33,19 @@ def tile_picked_siam_abs_p_kernel(
     nc = tc.nc
     with ExitStack() as ctx:
         keep = ctx.enter_context(tc.tile_pool(name="keep", bufs=1))
+        laid = ctx.enter_context(tc.tile_pool(name="laid", bufs=1))
         psum = ctx.enter_context(tc.psum_pool(name="psum", bufs=1))
 
         offsets = keep.tile([P, S // 16], U16, name="offsets")
         xs = keep.tile([P, T], U8, name="xs", align_bytes=64)
         xw = [keep.tile([P, T], U32, name="xw%d" % g, tag="xw%d" % g, align_bytes=64) for g in range(PASSES)]
-        raw = [keep.tile([P, PACK, H], F32, name="raw%d" % g, tag="raw%d" % g, align_bytes=64) for g in range(PASSES)]
+        raw = [
+            laid.tile([P, PACK, H], F32, name="raw0", offset=0, align_bytes=64),
+            keep.tile([P, PACK, H], F32, name="raw1", tag="raw1", align_bytes=64),
+        ]
         grouped = [
-            [keep.tile([P, H * 2], BF16, name="grouped%d_%d" % (g, h), align_bytes=64) for h in range(2)]
-            for g in range(PASSES)
+            [keep.tile([P, H * 2], BF16, name="grouped0_%d" % h, tag="grouped0_%d" % h, align_bytes=64) for h in range(2)],
+            [laid.tile([P, H * 2], BF16, name="grouped1_%d" % h, offset=H * 4 * h, align_bytes=64) for h in range(2)],
         ]
         w1c = [keep.tile([P, H], U32, name="w1c%d" % g, align_bytes=64) for g in range(PASSES)]
         w1s = [keep.tile([P, H], U8, name="w1s%d" % g, align_bytes=64) for g in range(PASSES)]
@@ -122,25 +127,28 @@ def tile_picked_siam_abs_p_kernel(
         for c, s in order:
             words[0, c, s] = gw0[:, columns(c, s)]
         nc.vector.tensor_copy(gs[:], xs[:].indirect(offsets[:]))
-        for h in range(2):
-            interleave(0, h, slice(0, P), h == 0)
-        w2w = keep.tile([P, N], U32, name="w2w", tag="raw0", align_bytes=64)
+        interleave(0, 0, slice(0, SHARE0), True)
+        interleave(0, 0, slice(SHARE0, P), False)
+        interleave(0, 1, slice(0, P), False)
+        w2w = laid.tile([P, N], U32, name="w2w", offset=H * 8, align_bytes=64)
         nc.sync.dma_start(out=w2w[:].bitcast(I32), in_=w2_words[0].rearrange("p n t -> p (n t)").bitcast(I32))
         load_w2_scales(range(1, 4))
         for t in range(2):
             quantize_w1(0, t * P, P, grouped[0][0][:, t * H : (t + 1) * H])
             for c, s in order:
                 product(0, c, s, t)
-        quantize_w1(0, HALF, HALF, grouped[0][1][:])
+        quantize_w1(0, 2 * P, P, grouped[0][1][:, :H])
         for c, s in order:
-            for t in (2, 3):
-                product(0, c, s, t)
+            product(0, c, s, 2)
 
         interleave(1, 0, slice(0, SHARE1), True)
         interleave(1, 0, slice(SHARE1, P), False)
         interleave(1, 1, slice(0, P), False)
+        quantize_w1(0, 3 * P, P, grouped[0][1][:, H:])
+        for c, s in order:
+            product(0, c, s, 3)
         quantize_w1(1, 0, HALF, grouped[1][0][:])
-        lead = keep.tile([P, 2 * C], U32, name="lead", align_bytes=64)
+        lead = keep.tile([P, 2 * C], U32, name="lead", tag="grouped0_1", align_bytes=64)
         for i, (c, s) in enumerate(order[:2]):
             gather_last_pass(lead[:, C * i : C * (i + 1)], c, s)
             for t in (0, 1):

@@ -24,7 +24,7 @@ HALF = H // 2
 SHARE0 = 84
 SHARE1 = 104
 TILES = (2, 4)
-PARTS = ((0, 128), (128, 64), (192, 64))
+PARTS = ((0, 64), (128, 64), (64, 64), (192, 64))
 
 
 def tile_picked_siam_abs_p_kernel(
@@ -195,7 +195,7 @@ def tile_picked_siam_abs_p_kernel(
 
         def absolute(c, at, n, on_vector=False):
             first = c * C + at
-            k = max(i for i, (lo, count) in enumerate(PARTS) if lo <= first)
+            k = min(i for i, (lo, count) in enumerate(PARTS) if lo <= first < lo + count)
             first = first - PARTS[k][0]
             dst = z[k][:, first * PACK : (first + n) * PACK]
             if on_vector:
@@ -215,7 +215,8 @@ def tile_picked_siam_abs_p_kernel(
         for at in range(0, 128, 32):
             relu(1, 0, at, 32, False)
             difference(1, 0, at, 32)
-        absolute(0, 0, 128)
+        absolute(0, 0, 64)
+        absolute(0, 64, 64)
         absolute(1, 0, 64, True)
         absolute(1, 64, 32)
         absolute(1, 96, 32)
@@ -226,7 +227,7 @@ def tile_picked_siam_abs_p_kernel(
             zc = keep.tile([P, n], U32, name="zc%d" % k, align_bytes=64)
             zs = keep.tile([P, n], U8, name="zs%d" % k, align_bytes=64)
             nc.vector.quantize_mx(out=zc[:].bitcast(FP8X4), scales=zs[:], in_=z[k][:])
-            acc = psum.tile([P, n], F32, name="acc%d" % k, tag=("b0_1_0", "b0_1_1", "b0_0_0")[k])
+            acc = psum.tile([P, n], F32, name="acc%d" % k, tag=("b0_1_0", "b0_1_1", "b0_0_0", "b0_0_1")[k])
             accs.append(acc)
             nc.tensor.matmul_mx(
                 out=acc[:],

@@ -21,7 +21,7 @@ PASSES = K // (P * PACK)
 C = 128
 CHUNKS = V // C
 HALF = H // 2
-SHARE0 = 84
+SHARE0 = 72
 SHARE1 = 104
 TILES = (2, 4)
 PARTS = ((0, 64), (128, 64), (64, 64), (192, 64))
@@ -37,7 +37,7 @@ def tile_picked_siam_abs_p_kernel(
         psum = ctx.enter_context(tc.psum_pool(name="psum", bufs=1))
 
         offsets = keep.tile([P, S // 16], U16, name="offsets")
-        xs = keep.tile([P, T], U8, name="xs", align_bytes=64)
+        xs = keep.tile([P, PASSES * T], U8, name="xs", align_bytes=64)
         xw = [keep.tile([P, T], U32, name="xw%d" % g, tag="xw%d" % g, align_bytes=64) for g in range(PASSES)]
         raw = [
             laid.tile([P, PACK, H], F32, name="raw0", offset=0, align_bytes=64),
@@ -50,7 +50,7 @@ def tile_picked_siam_abs_p_kernel(
         w1c = [keep.tile([P, H], U32, name="w1c%d" % g, align_bytes=64) for g in range(PASSES)]
         w1s = [keep.tile([P, H], U8, name="w1s%d" % g, align_bytes=64) for g in range(PASSES)]
         gw0 = keep.tile([P, S], U32, name="gw0", align_bytes=64)
-        gs = keep.tile([P, S], U8, name="gs", align_bytes=64)
+        gs = [keep.tile([P, S], U8, name="gs%d" % g, align_bytes=64) for g in range(PASSES)]
         w2s = keep.tile([P, N], U8, name="w2s", align_bytes=64)
 
         def load_w1(g):
@@ -68,14 +68,14 @@ def tile_picked_siam_abs_p_kernel(
                     in_=w2_scales[0, 4 * q : 4 * q + 4, :].bitcast(I32),
                 )
 
-        nc.gpsimd.memset(xs[:].bitcast(I32), 0)
+        nc.vector.memset(xs[:].bitcast(I32), 0)
         nc.gpsimd.memset(w2s[:].bitcast(I32), 0)
         load_x(0)
         nc.sync.dma_start(offsets[:], offs)
-        for q in range(4):
+        for r in range(4):
             nc.sync.dma_start(
-                out=xs[32 * q : 32 * q + 4 * PASSES, :].bitcast(I32),
-                in_=x_scales[:, 4 * q : 4 * q + 4, :].bitcast(I32),
+                out=xs[r:P:32, :].bitcast(I32).rearrange("q (g n) -> q g n", g=PASSES),
+                in_=x_scales[:, r:16:4, :].bitcast(I32).rearrange("g q n -> q g n"),
             )
         load_w2_scales(range(1))
         load_w1(0)
@@ -112,7 +112,7 @@ def tile_picked_siam_abs_p_kernel(
                 lhsT=w1c[g][:, chan].bitcast(FP8X4),
                 lhsT_scale=w1s[g][:, chan],
                 rhs=words[g, c, s].bitcast(FP8X4),
-                rhs_scale=gs[4 * g : P, columns(c, s)],
+                rhs_scale=gs[g][:, columns(c, s)],
                 start=(g == 0 and t % TILES[c] == 0),
                 stop=(g == PASSES - 1 and t % TILES[c] == TILES[c] - 1),
             )
@@ -126,10 +126,11 @@ def tile_picked_siam_abs_p_kernel(
         nc.vector.tensor_copy(gw0[:], xw[0][:].indirect(offsets[:]))
         for c, s in order:
             words[0, c, s] = gw0[:, columns(c, s)]
-        nc.vector.tensor_copy(gs[:], xs[:].indirect(offsets[:]))
-        interleave(0, 0, slice(0, SHARE0), True)
-        interleave(0, 0, slice(SHARE0, P), False)
-        interleave(0, 1, slice(0, P), False)
+        for g in range(PASSES):
+            nc.vector.tensor_copy(gs[g][:], xs[:, T * g : T * (g + 1)].indirect(offsets[:]))
+        interleave(0, 0, slice(0, P), False)
+        interleave(0, 1, slice(0, SHARE0), True)
+        interleave(0, 1, slice(SHARE0, P), False)
         w2w = laid.tile([P, N], U32, name="w2w", offset=H * 8, align_bytes=64)
         nc.sync.dma_start(out=w2w[:].bitcast(I32), in_=w2_words[0].rearrange("p n t -> p (n t)").bitcast(I32))
         load_w2_scales(range(1, 4))

@@ -164,9 +164,8 @@ def tile_picked_siam_abs_p_kernel(
             for t in range(PACK):
                 product(1, c, s, t)
 
-        w2 = keep.tile([P, N + N // PACK], I32, name="w2", tag="xw1", align_bytes=64)
-        nc.gpsimd.tensor_copy(out=w2[:, :N], in_=w2w[:].bitcast(I32))
-        nc.gpsimd.tensor_copy(out=w2[:, N:], in_=w2s[:].bitcast(I32))
+        w2p = keep.tile([P, N // PACK], I32, name="w2p", tag="xw1", align_bytes=64)
+        nc.gpsimd.tensor_copy(out=w2p[:], in_=w2s[:].bitcast(I32))
 
         diffs = [keep.tile([P, PACK // TILES[c], C, TILES[c]], BF16, name="diff%d" % c) for c in range(CHUNKS)]
         z = [keep.tile([P, n * PACK], BF16, name="z%d" % k, align_bytes=64) for k, (first, n) in enumerate(PARTS)]
@@ -232,8 +231,8 @@ def tile_picked_siam_abs_p_kernel(
             accs.append(acc)
             nc.tensor.matmul_mx(
                 out=acc[:],
-                lhsT=w2[:, :N].bitcast(FP8X4),
-                lhsT_scale=w2[:, N:].bitcast(U8),
+                lhsT=w2w[:].bitcast(FP8X4),
+                lhsT_scale=w2p[:].bitcast(U8),
                 rhs=zc[:].bitcast(FP8X4),
                 rhs_scale=zs[:],
                 start=True,

from contextlib import ExitStack

import concourse.mybir as mybir

K, T, S, V, H, N = 1024, 1024, 512, 256, 512, 128
FLOPS = 2 * K * H * S + 2 * H * N * V

F32 = mybir.dt.float32
BF16 = mybir.dt.bfloat16
I32 = mybir.dt.int32
U32 = mybir.dt.uint32
U16 = mybir.dt.uint16
U8 = mybir.dt.uint8
FP8X4 = mybir.dt.float8_e4m3fn_x4
ACT = mybir.ActivationFunctionType
ALU = mybir.AluOpType

P = 128
PACK = 4
PASSES = K // (P * PACK)
C = 128
CHUNKS = V // C
HALF = H // 2
SHARE0 = 72
SHARE1 = 104
TILES = (2, 4)
PARTS = ((0, 64), (128, 64), (64, 64), (192, 64))


def tile_picked_siam_abs_p_kernel(
    tc, x_words, x_scales, w1, w2_words, w2_scales, offs, out
):
    nc = tc.nc
    with ExitStack() as ctx:
        keep = ctx.enter_context(tc.tile_pool(name="keep", bufs=1))
        laid = ctx.enter_context(tc.tile_pool(name="laid", bufs=1))
        psum = ctx.enter_context(tc.psum_pool(name="psum", bufs=1))

        offsets = keep.tile([P, S // 16], U16, name="offsets")
        xs = keep.tile([P, PASSES * T], U8, name="xs", align_bytes=64)
        xw = [keep.tile([P, T], U32, name="xw%d" % g, tag="xw%d" % g, align_bytes=64) for g in range(PASSES)]
        raw = [
            laid.tile([P, PACK, H], F32, name="raw0", offset=0, align_bytes=64),
            keep.tile([P, PACK, H], F32, name="raw1", tag="raw1", align_bytes=64),
        ]
        grouped = [
            [keep.tile([P, H * 2], BF16, name="grouped0_%d" % h, tag="grouped0_%d" % h, align_bytes=64) for h in range(2)],
            [laid.tile([P, H * 2], BF16, name="grouped1_%d" % h, offset=H * 4 * h, align_bytes=64) for h in range(2)],
        ]
        w1c = [keep.tile([P, H], U32, name="w1c%d" % g, align_bytes=64) for g in range(PASSES)]
        w1s = [keep.tile([P, H], U8, name="w1s%d" % g, align_bytes=64) for g in range(PASSES)]
        gw0 = keep.tile([P, S], U32, name="gw0", align_bytes=64)
        gs = [keep.tile([P, S], U8, name="gs%d" % g, align_bytes=64) for g in range(PASSES)]
        w2s = keep.tile([P, N], U8, name="w2s", align_bytes=64)

        def load_w1(g):
            rows = w1[g * P * PACK : (g + 1) * P * PACK, :]
            nc.sync.dma_start(out=raw[g][:], in_=rows.rearrange("(p j) c -> p j c", j=PACK))

        def load_x(g):
            src = x_words[g].rearrange("p n t -> p (n t)").bitcast(I32)
            nc.sync.dma_start(out=xw[g][:].bitcast(I32), in_=src)

        def load_w2_scales(quadrants):
            for q in quadrants:
                nc.sync.dma_start(
                    out=w2s[32 * q : 32 * q + 4, :].bitcast(I32),
                    in_=w2_scales[0, 4 * q : 4 * q + 4, :].bitcast(I32),
                )

        nc.vector.memset(xs[:].bitcast(I32), 0)
        nc.gpsimd.memset(w2s[:].bitcast(I32), 0)
        load_x(0)
        nc.sync.dma_start(offsets[:], offs)
        for r in range(4):
            nc.sync.dma_start(
                out=xs[r:P:32, :].bitcast(I32).rearrange("q (g n) -> q g n", g=PASSES),
                in_=x_scales[:, r:16:4, :].bitcast(I32).rearrange("g q n -> q g n"),
            )
        load_w2_scales(range(1))
        load_w1(0)
        load_w1(1)
        load_x(1)

        def interleave(g, h, cols, on_vector):
            dst = grouped[g][h][:].rearrange("p (t m j) -> p m j t", t=2, j=PACK)[:, cols]
            src = raw[g][:].rearrange("p j (m t) -> p m j t", t=PACK)[:, cols, :, 2 * h : 2 * h + 2]
            if on_vector:
                nc.vector.tensor_copy(out=dst, in_=src)
            else:
                nc.scalar.activation(out=dst, in_=src, func=ACT.Copy)

        def quantize_w1(g, first, count, in_):
            cols = slice(first, first + count)
            nc.vector.quantize_mx(out=w1c[g][:, cols].bitcast(FP8X4), scales=w1s[g][:, cols], in_=in_)

        banks = {
            (c, s, h): psum.tile([P, TILES[c], C], F32, name="h%d_%d_%d" % (c, s, h), tag="b%d_%d_%d" % (c, s, h))
            for c in range(CHUNKS)
            for s in range(2)
            for h in range(PACK // TILES[c])
        }
        words = {}

        def columns(c, s):
            return slice(V * s + C * c, V * s + C * (c + 1))

        def product(g, c, s, t):
            chan = slice(P * t, P * (t + 1))
            nc.tensor.matmul_mx(
                out=banks[c, s, t // TILES[c]][:, t % TILES[c], :],
                lhsT=w1c[g][:, chan].bitcast(FP8X4),
                lhsT_scale=w1s[g][:, chan],
                rhs=words[g, c, s].bitcast(FP8X4),
                rhs_scale=gs[g][:, columns(c, s)],
                start=(g == 0 and t % TILES[c] == 0),
                stop=(g == PASSES - 1 and t % TILES[c] == TILES[c] - 1),
            )

        def gather_last_pass(dst, c, s):
            cols = columns(c, s)
            words[1, c, s] = dst
            nc.vector.tensor_copy(dst, xw[1][:].indirect(offsets[:, cols.start // 16 : cols.stop // 16]))

        order = [(c, s) for c in range(CHUNKS) for s in (1, 0)]
        nc.vector.tensor_copy(gw0[:], xw[0][:].indirect(offsets[:]))
        for c, s in order:
            words[0, c, s] = gw0[:, columns(c, s)]
        for g in range(PASSES):
            nc.vector.tensor_copy(gs[g][:], xs[:, T * g : T * (g + 1)].indirect(offsets[:]))
        interleave(0, 0, slice(0, P), False)
        interleave(0, 1, slice(0, SHARE0), True)
        interleave(0, 1, slice(SHARE0, P), False)
        w2w = laid.tile([P, N], U32, name="w2w", offset=H * 8, align_bytes=64)
        nc.sync.dma_start(out=w2w[:].bitcast(I32), in_=w2_words[0].rearrange("p n t -> p (n t)").bitcast(I32))
        load_w2_scales(range(1, 4))
        for t in range(2):
            quantize_w1(0, t * P, P, grouped[0][0][:, t * H : (t + 1) * H])
            for c, s in order:
                product(0, c, s, t)
        quantize_w1(0, 2 * P, P, grouped[0][1][:, :H])
        for c, s in order:
            product(0, c, s, 2)

        interleave(1, 0, slice(0, SHARE1), True)
        interleave(1, 0, slice(SHARE1, P), False)
        interleave(1, 1, slice(0, P), False)
        quantize_w1(0, 3 * P, P, grouped[0][1][:, H:])
        for c, s in order:
            product(0, c, s, 3)
        quantize_w1(1, 0, HALF, grouped[1][0][:])
        lead = keep.tile([P, 2 * C], U32, name="lead", tag="grouped0_1", align_bytes=64)
        for i, (c, s) in enumerate(order[:2]):
            gather_last_pass(lead[:, C * i : C * (i + 1)], c, s)
            for t in (0, 1):
                product(1, c, s, t)
        quantize_w1(1, HALF, HALF, grouped[1][1][:])
        for c, s in order[:2]:
            for t in (2, 3):
                product(1, c, s, t)
        rest = keep.tile([P, S - 2 * C], U32, name="rest", tag="raw1", align_bytes=64)
        for i, (c, s) in enumerate(order[2:]):
            gather_last_pass(rest[:, C * i : C * (i + 1)], c, s)
            for t in range(PACK):
                product(1, c, s, t)

        w2p = keep.tile([P, N // PACK], I32, name="w2p", tag="xw1", align_bytes=64)
        nc.gpsimd.tensor_copy(out=w2p[:], in_=w2s[:].bitcast(I32))

        diffs = [keep.tile([P, PACK // TILES[c], C, TILES[c]], BF16, name="diff%d" % c) for c in range(CHUNKS)]
        z = [keep.tile([P, n * PACK], BF16, name="z%d" % k, align_bytes=64) for k, (first, n) in enumerate(PARTS)]

        seconds = {
            (c, h): keep.tile([P, C, TILES[c]], F32, name="second%d_%d" % (c, h))
            for c in range(CHUNKS)
            for h in range(PACK // TILES[c])
        }

        def relu(c, h, at, n, on_vector):
            src = banks[c, 1, h][:, :, at : at + n].rearrange("p e v -> p v e")
            if on_vector:
                nc.vector.tensor_scalar_max(seconds[c, h][:, at : at + n, :], src, 0.0)
            else:
                nc.scalar.activation(out=seconds[c, h][:, at : at + n, :], in_=src, func=ACT.Relu)

        def difference(c, h, at, n):
            nc.vector.scalar_tensor_tensor(
                out=diffs[c][:, h, at : at + n, :],
                in0=banks[c, 0, h][:, :, at : at + n].rearrange("p e v -> p v e"),
                scalar=0.0,
                in1=seconds[c, h][:, at : at + n, :],
                op0=ALU.max,
                op1=ALU.subtract,
            )

        def absolute(c, at, n, on_vector=False):
            first = c * C + at
            k = min(i for i, (lo, count) in enumerate(PARTS) if lo <= first < lo + count)
            first = first - PARTS[k][0]
            dst = z[k][:, first * PACK : (first + n) * PACK]
            if on_vector:
                src = diffs[c][:, 0, at : at + n, :].rearrange("p v e -> p (v e)")
                nc.vector.scalar_tensor_tensor(out=dst, in0=src, scalar=-1.0, in1=src, op0=ALU.mult, op1=ALU.max)
            else:
                nc.scalar.activation(
                    out=dst.rearrange("p (v h e) -> p v h e", h=PACK // TILES[c], e=TILES[c]),
                    in_=diffs[c][:, :, at : at + n, :].rearrange("p h v e -> p v h e"),
                    func=ACT.Abs,
                )

        relu(0, 0, 0, 128, False)
        difference(0, 0, 0, 128)
        relu(0, 1, 0, 128, False)
        difference(0, 1, 0, 128)
        for at in range(0, 128, 32):
            relu(1, 0, at, 32, False)
            difference(1, 0, at, 32)
        absolute(0, 0, 64)
        absolute(0, 64, 64)
        absolute(1, 0, 64, True)
        absolute(1, 64, 32)
        absolute(1, 96, 32)

        res = [keep.tile([P, C], F32, name="res%d" % c) for c in range(CHUNKS)]
        accs = []
        for k, (first, n) in enumerate(PARTS):
            zc = keep.tile([P, n], U32, name="zc%d" % k, align_bytes=64)
            zs = keep.tile([P, n], U8, name="zs%d" % k, align_bytes=64)
            nc.vector.quantize_mx(out=zc[:].bitcast(FP8X4), scales=zs[:], in_=z[k][:])
            acc = psum.tile([P, n], F32, name="acc%d" % k, tag=("b0_1_0", "b0_1_1", "b0_0_0", "b0_0_1")[k])
            accs.append(acc)
            nc.tensor.matmul_mx(
                out=acc[:],
                lhsT=w2w[:].bitcast(FP8X4),
                lhsT_scale=w2p[:].bitcast(U8),
                rhs=zc[:].bitcast(FP8X4),
                rhs_scale=zs[:],
                start=True,
                stop=True,
            )
        for k, (first, n) in enumerate(PARTS):
            c, at = divmod(first, C)
            if c == 0:
                nc.scalar.copy(out=res[c][:, at : at + n], in_=accs[k][:])
            else:
                nc.vector.tensor_copy(out=res[c][:, at : at + n], in_=accs[k][:])
            if (first + n) % C == 0:
                nc.sync.dma_start(out=out[:, C * c : C * (c + 1)], in_=res[c][:])
